import numpy as np, ml_dtypes
CORES = [22,46,70,150,174,198,278,302,326,406,430,454]
N = 12
TK = 128
def setup_inputs(rng):
    return {"b": rng.standard_normal((N, 128, TK), dtype=np.float32).astype(ml_dtypes.bfloat16), "l": (rng.standard_normal((N, 128, N * 128), dtype=np.float32) / 16).astype(ml_dtypes.bfloat16)}
def setup_inputs_big(rng):
    d = setup_inputs(rng)
    for k in ("b",): d[k] = (d[k].astype(np.float32) * 1048576.0).astype(d[k].dtype)
    return d
def setup_inputs_small(rng):
    d = setup_inputs(rng)
    for k in ("b",): d[k] = (d[k].astype(np.float32) * (1 / 1048576.0)).astype(d[k].dtype)
    return d
def setup_inputs_apart(rng):
    d = setup_inputs(rng)
    f = (10.0 ** rng.permutation(np.linspace(-1.5, 1.5, N))).astype(np.float32).reshape(N, 1, 1)
    for k in ("b",): d[k] = (d[k].astype(np.float32) * f).astype(d[k].dtype)
    return d
def reference(b, l):
    B, L = b.astype(np.float64), l.astype(np.float64)
    y = np.zeros((N, 128, TK))
    for r in range(N):
        acc = B[r].copy()
        for s in range(r):
            acc -= L[r][:, 128 * s:128 * s + 128].T @ y[s]
        y[r] = acc
    return {"y": y.astype(ml_dtypes.bfloat16)}

@@ -1,0 +1,157 @@
+from concourse.bass import DstId, RemoteDMATransfer
+from concourse.mybir import AluOpType
+
+N = 12
+W = 128
+NS = 6
+_SLOTW = [max(1 + r for r in range(N) if r % NS == k) for k in range(NS)]
+_SLOTO = [sum(_SLOTW[:k]) for k in range(NS)]
+
+SCRATCH = {
+    "rows": ("sbuf", [128, sum(_SLOTW) * W], "bfloat16"),
+    "ybuf": ("sbuf", [128, N * W], "bfloat16"),
+}
+for _k in range(NS):
+    SCRATCH["ps%d" % _k] = ("psum", [128, 512], "float32")
+
+SEMAPHORES = (["ld", "st", "snt"] + ["row%d" % k for k in range(NS)] + ["pa%d" % k for k in range(NS)]
+              + ["yv%d" % k for k in range(NS)] + ["yg%d" % k for k in range(4)])
+
+
+def _plan(cores, topo):
+    groups = []
+    for r in range(len(cores)):
+        if groups and topo.host(cores[groups[-1][0]]) == topo.host(cores[r]):
+            groups[-1].append(r)
+        else:
+            groups.append([r])
+    last = len(groups) - 1
+    solve, grp = {}, {}
+    for gi, mem in enumerate(groups):
+        for p in mem:
+            grp[p] = gi
+            if gi == 0 or gi == last:
+                solve[p] = (mem[0], p)
+            elif gi == 1:
+                solve[p] = (groups[0][0], mem[-1])
+            else:
+                solve[p] = (mem[0], mem[-1])
+    ymsg = []
+    for t in range(2, len(groups)):
+        for s in range(t):
+            holder = groups[s][-1]
+            if s < t - 1 and all(topo.may_write(cores[holder], cores[q]) for q in groups[t]):
+                ymsg.append((holder, list(groups[t]), s))
+            else:
+                for q in groups[t]:
+                    pred = [p for p in groups[t - 1] if topo.chip(cores[p]) == topo.chip(cores[q])][0]
+                    ymsg.append((pred, [q], s))
+    return groups, grp, solve, ymsg
+
+
+def rank_program(g, core, T, topo):
+    me = T.rank_of(core)
+    if me is None:
+        return
+    cores = T.cores
+    groups, grp, solve, ymsg = _plan(cores, topo)
+    lo, hi = solve[me]
+    sem = T.sem
+
+    def engines(src, dsts):
+        m = topo.mask(cores[src], cores[dsts[0]])
+        for d in dsts[1:]:
+            m &= topo.mask(cores[src], cores[d])
+        return m, bin(m).count("1")
+
+    def yblk(a, b):
+        return T.ybuf[:, a * W:b * W]
+
+    def rowcols(r, a, b):
+        o = _SLOTO[r % NS]
+        return T.rows[:, (o + a) * W:(o + b) * W]
+
+    def row_calls(r):
+        dst = [p for p in range(len(cores)) if p != r and solve[p][0] <= r <= solve[p][1]]
+        far = [p for p in dst if grp[p] != grp[r]]
+        near = [p for p in dst if grp[p] == grp[r]]
+        return [c for c in (far, near) if c]
+
+    def row_cond(r):
+        if r == me:
+            return ("ld", 16 if r == 0 else 32)
+        call = [c for c in row_calls(r) if me in c][0]
+        return ("row%d" % (r % NS), engines(r, call)[1])
+
+    def y_cond(s):
+        if lo <= s <= hi:
+            return row_cond(0) if s == 0 else ("yv%d" % (s % NS), 1)
+        src, dsts = [(a, d) for (a, d, gs) in ymsg if gs == grp[s] and me in d][0]
+        return ("yg%d" % grp[s], engines(src, dsts)[1])
+
+    total = {}
+    seen = set()
+
+    def need(qname, q, cond):
+        total[cond[0]] = max(total.get(cond[0], 0), cond[1])
+        if (qname, cond) not in seen:
+            seen.add((qname, cond))
+            q.wait_ge(sem[cond[0]], cond[1])
+
+    if me == 0:
+        g.sync.dma_start(yblk(0, 1), T.b[:, :]).then_inc(sem.ld, 16)
+    else:
+        g.sync.dma_start(rowcols(me, 0, 1), T.b[:, :]).then_inc(sem.ld, 16)
+        g.scalar.dma_start(rowcols(me, 1, 1 + me), T.l[:, 0:me * W]).then_inc(sem.ld, 16)
+
+    ext = [s for s in range(len(groups)) if groups[s][-1] < lo]
+    rows = [r for r in range(lo, hi + 1) if r > 0]
+    order = []
+    for s in ext[:-1]:
+        order += [(r, c) for r in rows for c in groups[s]]
+    tail = list(groups[ext[-1]]) if ext else []
+    for r in rows:
+        order += [(r, c) for c in tail + list(range(lo, r))]
+    done = {}
+    for (r, c) in order:
+        need("t", g.tensor, row_cond(r))
+        need("t", g.tensor, y_cond(c))
+        k = done.get(r, 0)
+        done[r] = k + 1
+        g.tensor.matmul(T["ps%d" % (r % NS)][:, 0:W], rowcols(r, 1 + c, 2 + c), yblk(c, c + 1),
+                        k == 0, k + 1 == r).then_inc(sem["pa%d" % (r % NS)], 1)
+
+    for r in rows:
+        need("v", g.vector, ("pa%d" % (r % NS), r))
+        need("v", g.vector, row_cond(r))
+        g.vector.tensor_tensor(yblk(r, r + 1), rowcols(r, 0, 1), T["ps%d" % (r % NS)][:, 0:W],
+                               AluOpType.subtract).then_inc(sem["yv%d" % (r % NS)], 1)
+
+    need("s", g.sync, y_cond(me))
+    g.sync.dma_start(T.y[:, :], yblk(me, me + 1)).then_inc(sem.st, 16)
+    total["st"] = 16
+
+    sent = [0]
+
+    def send(dsts, ap, rsem):
+        m, ne = engines(me, dsts)
+        ids = []
+        for d in dsts:
+            rid, pid = topo.addr(cores[d], core)
+            ids.append(DstId(rid=rid, pnc=pid))
+        g.remote_dma_fused([RemoteDMATransfer(dst_ids=ids, dma_engine_mask=m, remote_sem=sem[rsem],
+                                              srcs=[ap], dsts=[ap for _ in dsts], alu_op=0)], local_sem=sem.snt)
+        sent[0] += ne
+
+    for call in row_calls(me):
+        need("g", g, row_cond(me))
+        send(call, yblk(0, 1) if me == 0 else rowcols(me, 0, 1 + me), "row%d" % (me % NS))
+    for (src, dsts, s) in sorted([m for m in ymsg if m[0] == me], key=lambda m: m[2]):
+        for c in groups[s]:
+            need("g", g, y_cond(c))
+        send(dsts, yblk(groups[s][0], groups[s][-1] + 1), "yg%d" % s)
+
+    if sent[0]:
+        total["snt"] = sent[0]
+    for name in sorted(total):
+        need("g", g, (name, total[name]))

@@ -10,12 +10,17 @@ _SLOTO = [sum(_SLOTW[:k]) for k in range(NS)]
 SCRATCH = {
     "rows": ("sbuf", [128, sum(_SLOTW) * W], "bfloat16"),
     "ybuf": ("sbuf", [128, N * W], "bfloat16"),
+    "trow": ("sbuf", [128, N * W], "bfloat16"),
+    "ones": ("sbuf", [128, W], "bfloat16"),
+    "ident": ("sbuf", [128, W], "bfloat16"),
+    "tpa": ("psum", [128, 8 * W], "bfloat16"),
+    "tpb": ("psum", [128, 8 * W], "bfloat16"),
 }
 for _k in range(NS):
     SCRATCH["ps%d" % _k] = ("psum", [128, 512], "float32")
 
-SEMAPHORES = (["ld", "st", "snt"] + ["row%d" % k for k in range(NS)] + ["pa%d" % k for k in range(NS)]
-              + ["yv%d" % k for k in range(NS)] + ["yg%d" % k for k in range(4)])
+SEMAPHORES = (["ld", "ld2", "st", "snt", "idn", "tpa", "tpb", "tc", "ef"] + ["row%d" % k for k in range(NS)]
+              + ["pa%d" % k for k in range(NS)] + ["yv%d" % k for k in range(NS)] + ["yg%d" % k for k in range(4)])
 
 
 def _plan(cores, topo):
@@ -55,7 +60,9 @@ def rank_program(g, core, T, topo):
         return
     cores = T.cores
     groups, grp, solve, ymsg = _plan(cores, topo)
-    lo, hi = solve[me]
+    last = len(groups) - 1
+    fold = grp[me] == last
+    lo, hi = (me, me) if fold else solve[me]
     sem = T.sem
 
     def engines(src, dsts):
@@ -75,6 +82,8 @@ def rank_program(g, core, T, topo):
         dst = [p for p in range(len(cores)) if p != r and solve[p][0] <= r <= solve[p][1]]
         far = [p for p in dst if grp[p] != grp[r]]
         near = [p for p in dst if grp[p] == grp[r]]
+        if grp[r] == last:
+            near = near[::-1]
         return [c for c in (far, near) if c]
 
     def row_cond(r):
@@ -104,28 +113,96 @@ def rank_program(g, core, T, topo):
         g.sync.dma_start(rowcols(me, 0, 1), T.b[:, :]).then_inc(sem.ld, 16)
         g.scalar.dma_start(rowcols(me, 1, 1 + me), T.l[:, 0:me * W]).then_inc(sem.ld, 16)
 
-    ext = [s for s in range(len(groups)) if groups[s][-1] < lo]
-    rows = [r for r in range(lo, hi + 1) if r > 0]
-    order = []
-    for s in ext[:-1]:
-        order += [(r, c) for r in rows for c in groups[s]]
-    tail = list(groups[ext[-1]]) if ext else []
-    for r in rows:
-        order += [(r, c) for c in tail + list(range(lo, r))]
-    done = {}
-    for (r, c) in order:
-        need("t", g.tensor, row_cond(r))
-        need("t", g.tensor, y_cond(c))
-        k = done.get(r, 0)
-        done[r] = k + 1
-        g.tensor.matmul(T["ps%d" % (r % NS)][:, 0:W], rowcols(r, 1 + c, 2 + c), yblk(c, c + 1),
-                        k == 0, k + 1 == r).then_inc(sem["pa%d" % (r % NS)], 1)
+    ships_t = fold and bool(row_calls(me))
 
-    for r in rows:
-        need("v", g.vector, ("pa%d" % (r % NS), r))
-        need("v", g.vector, row_cond(r))
-        g.vector.tensor_tensor(yblk(r, r + 1), rowcols(r, 0, 1), T["ps%d" % (r % NS)][:, 0:W],
-                               AluOpType.subtract).then_inc(sem["yv%d" % (r % NS)], 1)
+    if not fold:
+        ext = [s for s in range(len(groups)) if groups[s][-1] < lo]
+        rows = [r for r in range(lo, hi + 1) if r > 0]
+        order = []
+        for s in ext[:-1]:
+            order += [(r, c) for r in rows for c in groups[s]]
+        tail = list(groups[ext[-1]]) if ext else []
+        for r in rows:
+            order += [(r, c) for c in tail + list(range(lo, r))]
+        done = {}
+        for (r, c) in order:
+            need("t", g.tensor, row_cond(r))
+            need("t", g.tensor, y_cond(c))
+            k = done.get(r, 0)
+            done[r] = k + 1
+            g.tensor.matmul(T["ps%d" % (r % NS)][:, 0:W], rowcols(r, 1 + c, 2 + c), yblk(c, c + 1),
+                            k == 0, k + 1 == r).then_inc(sem["pa%d" % (r % NS)], 1)
+
+        for r in rows:
+            need("v", g.vector, ("pa%d" % (r % NS), r))
+            need("v", g.vector, row_cond(r))
+            g.vector.tensor_tensor(yblk(r, r + 1), rowcols(r, 0, 1), T["ps%d" % (r % NS)][:, 0:W],
+                                   AluOpType.subtract).then_inc(sem["yv%d" % (r % NS)], 1)
+    else:
+        g0 = groups[last][0]
+        prev = list(range(g0, me))
+        if ships_t:
+            g.sync.dma_start(T.trow[:, 0:W], T.b[:, :]).then_inc(sem.ld2, 16)
+            g.vector.memset(T.ones[:, :], 1.0).then_inc(sem.idn, 1)
+            need("g", g, ("idn", 1))
+            g.affine_select(T.ident[:, :], T.ones[:, :], [[-1, W]], AluOpType.is_equal, 0.0, 0, 1).then_inc(sem.idn, 1)
+            half = (me + 1) // 2
+            banks = [(nm, ss) for (nm, ss) in (("tpa", list(range(0, half))), ("tpb", list(range(half, me)))) if ss]
+            need("t", g.tensor, row_cond(me))
+            need("t", g.tensor, ("idn", 2))
+            for nm, ss in banks:
+                for k, s in enumerate(ss):
+                    g.tensor.transpose(T[nm][:, k * W:(k + 1) * W], rowcols(me, 1 + s, 2 + s),
+                                       T.ident[:, :]).then_inc(sem[nm], 1)
+            for nm, ss in banks:
+                need("v", g.vector, (nm, len(ss)))
+                g.vector.tensor_copy(T.trow[:, (1 + ss[0]) * W:(2 + ss[-1]) * W],
+                                     T[nm][:, 0:len(ss) * W]).then_inc(sem.tc, 1)
+            ntc = len(banks)
+        nef = 0
+        if prev:
+            need("t", g.tensor, row_cond(me))
+            need("v", g.vector, row_cond(me))
+            for p in prev:
+                need("t", g.tensor, row_cond(p))
+            npa = 0
+            for s in range(me - 2, g0 - 1, -1):
+                ps = list(range(s + 1, me))
+                if nef:
+                    need("t", g.tensor, ("ef", nef))
+                for k, p in enumerate(ps):
+                    g.tensor.matmul(T.ps3[:, 0:W], rowcols(p, 1 + s, 2 + s), rowcols(me, 1 + p, 2 + p),
+                                    k == 0, k + 1 == len(ps)).then_inc(sem.pa3, 1)
+                npa += len(ps)
+                need("v", g.vector, ("pa3", npa))
+                g.vector.tensor_tensor(rowcols(me, 1 + s, 2 + s), rowcols(me, 1 + s, 2 + s), T.ps3[:, 0:W],
+                                       AluOpType.subtract).then_inc(sem.ef, 1)
+                nef += 1
+            if nef:
+                need("t", g.tensor, ("ef", nef))
+            chunks = [list(range(a, min(a + 4, g0))) for a in range(0, g0, 4)]
+            for ci, ss in enumerate(chunks):
+                for k, s in enumerate(ss):
+                    for kk, p in enumerate(prev):
+                        g.tensor.matmul(T["ps%d" % ci][:, k * W:(k + 1) * W], rowcols(p, 1 + s, 2 + s),
+                                        rowcols(me, 1 + p, 2 + p), kk == 0,
+                                        kk + 1 == len(prev)).then_inc(sem["pa%d" % ci], 1)
+                need("v", g.vector, ("pa%d" % ci, len(ss) * len(prev)))
+                g.vector.tensor_tensor(rowcols(me, 1 + ss[0], 2 + ss[-1]), rowcols(me, 1 + ss[0], 2 + ss[-1]),
+                                       T["ps%d" % ci][:, 0:len(ss) * W], AluOpType.subtract).then_inc(sem.ef, 1)
+                nef += 1
+            need("t", g.tensor, ("ef", nef))
+        need("t", g.tensor, row_cond(me))
+        terms = [(p, rowcols(p, 0, 1), None) for p in prev] + [(s, yblk(s, s + 1), y_cond(s)) for s in range(g0)]
+        for k, (c, rhs, cond) in enumerate(terms):
+            if cond is not None:
+                need("t", g.tensor, cond)
+            g.tensor.matmul(T.ps4[:, 0:W], rowcols(me, 1 + c, 2 + c), rhs, k == 0,
+                            k + 1 == len(terms)).then_inc(sem.pa4, 1)
+        need("v", g.vector, ("pa4", len(terms)))
+        need("v", g.vector, row_cond(me))
+        g.vector.tensor_tensor(yblk(me, me + 1), rowcols(me, 0, 1), T.ps4[:, 0:W],
+                               AluOpType.subtract).then_inc(sem["yv%d" % (me % NS)], 1)
 
     need("s", g.sync, y_cond(me))
     g.sync.dma_start(T.y[:, :], yblk(me, me + 1)).then_inc(sem.st, 16)
@@ -133,23 +210,29 @@ def rank_program(g, core, T, topo):
 
     sent = [0]
 
-    def send(dsts, ap, rsem):
+    def send(dsts, src, dst, rsem):
         m, ne = engines(me, dsts)
         ids = []
         for d in dsts:
             rid, pid = topo.addr(cores[d], core)
             ids.append(DstId(rid=rid, pnc=pid))
         g.remote_dma_fused([RemoteDMATransfer(dst_ids=ids, dma_engine_mask=m, remote_sem=sem[rsem],
-                                              srcs=[ap], dsts=[ap for _ in dsts], alu_op=0)], local_sem=sem.snt)
+                                              srcs=[src], dsts=[dst for _ in dsts], alu_op=0)], local_sem=sem.snt)
         sent[0] += ne
 
     for call in row_calls(me):
-        need("g", g, row_cond(me))
-        send(call, yblk(0, 1) if me == 0 else rowcols(me, 0, 1 + me), "row%d" % (me % NS))
+        if ships_t:
+            need("g", g, ("tc", ntc))
+            need("g", g, ("ld2", 16))
+            send(call, T.trow[:, 0:(1 + me) * W], rowcols(me, 0, 1 + me), "row%d" % (me % NS))
+        else:
+            need("g", g, row_cond(me))
+            ap = yblk(0, 1) if me == 0 else rowcols(me, 0, 1 + me)
+            send(call, ap, ap, "row%d" % (me % NS))
     for (src, dsts, s) in sorted([m for m in ymsg if m[0] == me], key=lambda m: m[2]):
         for c in groups[s]:
             need("g", g, y_cond(c))
-        send(dsts, yblk(groups[s][0], groups[s][-1] + 1), "yg%d" % s)
+        send(dsts, yblk(groups[s][0], groups[s][-1] + 1), yblk(groups[s][0], groups[s][-1] + 1), "yg%d" % s)
 
     if sent[0]:
         total["snt"] = sent[0]

from concourse.bass import DstId, RemoteDMATransfer
from concourse.mybir import AluOpType

N = 12
W = 128
NS = 6
_SLOTW = [max(1 + r for r in range(N) if r % NS == k) for k in range(NS)]
_SLOTO = [sum(_SLOTW[:k]) for k in range(NS)]

SCRATCH = {
    "rows": ("sbuf", [128, sum(_SLOTW) * W], "bfloat16"),
    "ybuf": ("sbuf", [128, N * W], "bfloat16"),
    "trow": ("sbuf", [128, N * W], "bfloat16"),
    "ones": ("sbuf", [128, W], "bfloat16"),
    "ident": ("sbuf", [128, W], "bfloat16"),
    "tpa": ("psum", [128, 8 * W], "bfloat16"),
    "tpb": ("psum", [128, 8 * W], "bfloat16"),
}
for _k in range(NS):
    SCRATCH["ps%d" % _k] = ("psum", [128, 512], "float32")

SEMAPHORES = (["ld", "ld2", "st", "snt", "idn", "tpa", "tpb", "tc", "ef"] + ["row%d" % k for k in range(NS)]
              + ["pa%d" % k for k in range(NS)] + ["yv%d" % k for k in range(NS)] + ["yg%d" % k for k in range(4)])


def _plan(cores, topo):
    groups = []
    for r in range(len(cores)):
        if groups and topo.host(cores[groups[-1][0]]) == topo.host(cores[r]):
            groups[-1].append(r)
        else:
            groups.append([r])
    last = len(groups) - 1
    solve, grp = {}, {}
    for gi, mem in enumerate(groups):
        for p in mem:
            grp[p] = gi
            if gi == 0 or gi == last:
                solve[p] = (mem[0], p)
            elif gi == 1:
                solve[p] = (groups[0][0], mem[-1])
            else:
                solve[p] = (mem[0], mem[-1])
    ymsg = []
    for t in range(2, len(groups)):
        for s in range(t):
            holder = groups[s][-1]
            if s < t - 1 and all(topo.may_write(cores[holder], cores[q]) for q in groups[t]):
                ymsg.append((holder, list(groups[t]), s))
            else:
                for q in groups[t]:
                    pred = [p for p in groups[t - 1] if topo.chip(cores[p]) == topo.chip(cores[q])][0]
                    ymsg.append((pred, [q], s))
    return groups, grp, solve, ymsg


def rank_program(g, core, T, topo):
    me = T.rank_of(core)
    if me is None:
        return
    cores = T.cores
    groups, grp, solve, ymsg = _plan(cores, topo)
    last = len(groups) - 1
    fold = grp[me] == last
    lo, hi = (me, me) if fold else solve[me]
    sem = T.sem

    def engines(src, dsts):
        m = topo.mask(cores[src], cores[dsts[0]])
        for d in dsts[1:]:
            m &= topo.mask(cores[src], cores[d])
        return m, bin(m).count("1")

    def yblk(a, b):
        return T.ybuf[:, a * W:b * W]

    def rowcols(r, a, b):
        o = _SLOTO[r % NS]
        return T.rows[:, (o + a) * W:(o + b) * W]

    def row_calls(r):
        dst = [p for p in range(len(cores)) if p != r and solve[p][0] <= r <= solve[p][1]]
        far = [p for p in dst if grp[p] != grp[r]]
        near = [p for p in dst if grp[p] == grp[r]]
        if grp[r] == last:
            near = near[::-1]
        return [c for c in (far, near) if c]

    def row_cond(r):
        if r == me:
            return ("ld", 16 if r == 0 else 32)
        call = [c for c in row_calls(r) if me in c][0]
        return ("row%d" % (r % NS), engines(r, call)[1])

    def y_cond(s):
        if lo <= s <= hi:
            return row_cond(0) if s == 0 else ("yv%d" % (s % NS), 1)
        src, dsts = [(a, d) for (a, d, gs) in ymsg if gs == grp[s] and me in d][0]
        return ("yg%d" % grp[s], engines(src, dsts)[1])

    total = {}
    seen = set()

    def need(qname, q, cond):
        total[cond[0]] = max(total.get(cond[0], 0), cond[1])
        if (qname, cond) not in seen:
            seen.add((qname, cond))
            q.wait_ge(sem[cond[0]], cond[1])

    if me == 0:
        g.sync.dma_start(yblk(0, 1), T.b[:, :]).then_inc(sem.ld, 16)
    else:
        g.sync.dma_start(rowcols(me, 0, 1), T.b[:, :]).then_inc(sem.ld, 16)
        g.scalar.dma_start(rowcols(me, 1, 1 + me), T.l[:, 0:me * W]).then_inc(sem.ld, 16)

    ships_t = fold and bool(row_calls(me))

    if not fold:
        ext = [s for s in range(len(groups)) if groups[s][-1] < lo]
        rows = [r for r in range(lo, hi + 1) if r > 0]
        order = []
        for s in ext[:-1]:
            order += [(r, c) for r in rows for c in groups[s]]
        tail = list(groups[ext[-1]]) if ext else []
        for r in rows:
            order += [(r, c) for c in tail + list(range(lo, r))]
        done = {}
        for (r, c) in order:
            need("t", g.tensor, row_cond(r))
            need("t", g.tensor, y_cond(c))
            k = done.get(r, 0)
            done[r] = k + 1
            g.tensor.matmul(T["ps%d" % (r % NS)][:, 0:W], rowcols(r, 1 + c, 2 + c), yblk(c, c + 1),
                            k == 0, k + 1 == r).then_inc(sem["pa%d" % (r % NS)], 1)

        for r in rows:
            need("v", g.vector, ("pa%d" % (r % NS), r))
            need("v", g.vector, row_cond(r))
            g.vector.tensor_tensor(yblk(r, r + 1), rowcols(r, 0, 1), T["ps%d" % (r % NS)][:, 0:W],
                                   AluOpType.subtract).then_inc(sem["yv%d" % (r % NS)], 1)
    else:
        g0 = groups[last][0]
        prev = list(range(g0, me))
        if ships_t:
            g.sync.dma_start(T.trow[:, 0:W], T.b[:, :]).then_inc(sem.ld2, 16)
            g.vector.memset(T.ones[:, :], 1.0).then_inc(sem.idn, 1)
            need("g", g, ("idn", 1))
            g.affine_select(T.ident[:, :], T.ones[:, :], [[-1, W]], AluOpType.is_equal, 0.0, 0, 1).then_inc(sem.idn, 1)
            half = (me + 1) // 2
            banks = [(nm, ss) for (nm, ss) in (("tpa", list(range(0, half))), ("tpb", list(range(half, me)))) if ss]
            need("t", g.tensor, row_cond(me))
            need("t", g.tensor, ("idn", 2))
            for nm, ss in banks:
                for k, s in enumerate(ss):
                    g.tensor.transpose(T[nm][:, k * W:(k + 1) * W], rowcols(me, 1 + s, 2 + s),
                                       T.ident[:, :]).then_inc(sem[nm], 1)
            for nm, ss in banks:
                need("v", g.vector, (nm, len(ss)))
                g.vector.tensor_copy(T.trow[:, (1 + ss[0]) * W:(2 + ss[-1]) * W],
                                     T[nm][:, 0:len(ss) * W]).then_inc(sem.tc, 1)
            ntc = len(banks)
        nef = 0
        if prev:
            need("t", g.tensor, row_cond(me))
            need("v", g.vector, row_cond(me))
            for p in prev:
                need("t", g.tensor, row_cond(p))
            npa = 0
            for s in range(me - 2, g0 - 1, -1):
                ps = list(range(s + 1, me))
                if nef:
                    need("t", g.tensor, ("ef", nef))
                for k, p in enumerate(ps):
                    g.tensor.matmul(T.ps3[:, 0:W], rowcols(p, 1 + s, 2 + s), rowcols(me, 1 + p, 2 + p),
                                    k == 0, k + 1 == len(ps)).then_inc(sem.pa3, 1)
                npa += len(ps)
                need("v", g.vector, ("pa3", npa))
                g.vector.tensor_tensor(rowcols(me, 1 + s, 2 + s), rowcols(me, 1 + s, 2 + s), T.ps3[:, 0:W],
                                       AluOpType.subtract).then_inc(sem.ef, 1)
                nef += 1
            if nef:
                need("t", g.tensor, ("ef", nef))
            chunks = [list(range(a, min(a + 4, g0))) for a in range(0, g0, 4)]
            for ci, ss in enumerate(chunks):
                for k, s in enumerate(ss):
                    for kk, p in enumerate(prev):
                        g.tensor.matmul(T["ps%d" % ci][:, k * W:(k + 1) * W], rowcols(p, 1 + s, 2 + s),
                                        rowcols(me, 1 + p, 2 + p), kk == 0,
                                        kk + 1 == len(prev)).then_inc(sem["pa%d" % ci], 1)
                need("v", g.vector, ("pa%d" % ci, len(ss) * len(prev)))
                g.vector.tensor_tensor(rowcols(me, 1 + ss[0], 2 + ss[-1]), rowcols(me, 1 + ss[0], 2 + ss[-1]),
                                       T["ps%d" % ci][:, 0:len(ss) * W], AluOpType.subtract).then_inc(sem.ef, 1)
                nef += 1
            need("t", g.tensor, ("ef", nef))
        need("t", g.tensor, row_cond(me))
        terms = [(p, rowcols(p, 0, 1), None) for p in prev] + [(s, yblk(s, s + 1), y_cond(s)) for s in range(g0)]
        for k, (c, rhs, cond) in enumerate(terms):
            if cond is not None:
                need("t", g.tensor, cond)
            g.tensor.matmul(T.ps4[:, 0:W], rowcols(me, 1 + c, 2 + c), rhs, k == 0,
                            k + 1 == len(terms)).then_inc(sem.pa4, 1)
        need("v", g.vector, ("pa4", len(terms)))
        need("v", g.vector, row_cond(me))
        g.vector.tensor_tensor(yblk(me, me + 1), rowcols(me, 0, 1), T.ps4[:, 0:W],
                               AluOpType.subtract).then_inc(sem["yv%d" % (me % NS)], 1)

    need("s", g.sync, y_cond(me))
    g.sync.dma_start(T.y[:, :], yblk(me, me + 1)).then_inc(sem.st, 16)
    total["st"] = 16

    sent = [0]

    def send(dsts, src, dst, rsem):
        m, ne = engines(me, dsts)
        ids = []
        for d in dsts:
            rid, pid = topo.addr(cores[d], core)
            ids.append(DstId(rid=rid, pnc=pid))
        g.remote_dma_fused([RemoteDMATransfer(dst_ids=ids, dma_engine_mask=m, remote_sem=sem[rsem],
                                              srcs=[src], dsts=[dst for _ in dsts], alu_op=0)], local_sem=sem.snt)
        sent[0] += ne

    for call in row_calls(me):
        if ships_t:
            need("g", g, ("tc", ntc))
            need("g", g, ("ld2", 16))
            send(call, T.trow[:, 0:(1 + me) * W], rowcols(me, 0, 1 + me), "row%d" % (me % NS))
        else:
            need("g", g, row_cond(me))
            ap = yblk(0, 1) if me == 0 else rowcols(me, 0, 1 + me)
            send(call, ap, ap, "row%d" % (me % NS))
    for (src, dsts, s) in sorted([m for m in ymsg if m[0] == me], key=lambda m: m[2]):
        for c in groups[s]:
            need("g", g, y_cond(c))
        send(dsts, yblk(groups[s][0], groups[s][-1] + 1), yblk(groups[s][0], groups[s][-1] + 1), "yg%d" % s)

    if sent[0]:
        total["snt"] = sent[0]
    for name in sorted(total):
        need("g", g, (name, total[name]))
